import numpy as np
import ml_dtypes


def mxq(x, axis, fmt="e4m3"):
    dtype, down = {"e4m3": (ml_dtypes.float8_e4m3fn, 7), "e5m2": (ml_dtypes.float8_e5m2, 14)}[fmt]
    v = np.moveaxis(np.asarray(x, np.float32).astype(ml_dtypes.bfloat16).astype(np.float64), axis, -1)
    blocks = v.reshape(v.shape[:-1] + (-1, 32))
    amax = np.abs(blocks).max(-1, keepdims=True)
    byte = np.maximum(np.where(amax > 0, np.frexp(amax)[1] - 1 + 127, 0) - down, 1)
    scale = np.exp2(byte - 127.0)
    codes = (blocks / scale).astype(np.float32).astype(dtype).astype(np.float64)
    return np.moveaxis((codes * scale).reshape(v.shape), -1, axis)


WIDE = False


def mx_kscale(k):
    if not WIDE:
        return np.ones(k)
    levels = np.array([30, -30])
    if k % 512:
        return np.exp2(np.random.permutation(np.resize(levels, k // 32))).repeat(32)
    a = np.empty((k // 512, 16))
    for p in range(k // 512):
        a[p, :8] = np.random.permutation(np.resize(levels, 8))
        for g in range(8):
            far = levels[np.abs(levels - a[p, g]) >= 10]
            a[p, g + 8] = far[np.random.randint(len(far))]
    return np.exp2(a.ravel()).repeat(32)


def f64(x):
    return np.asarray(x).astype(np.float64)


def striped(idx):
    return np.tile(np.asarray(idx).reshape(-1, 16).T, (8, 1)).astype(np.uint16)


def unstriped(offs):
    return offs[:16].T.reshape(-1).astype(np.int64)


E2M1 = np.array([0.0, 0.5, 1.0, 1.5, 2.0, 3.0, 4.0, 6.0, -0.0, -0.5, -1.0, -1.5, -2.0, -3.0, -4.0, -6.0])


def pack_weight(w, fmt):
    k, n = w.shape
    w = f64(np.asarray(w, np.float32).astype(ml_dtypes.bfloat16)).reshape(k // 32, 32, n)
    amax = np.abs(w).max(1)
    if fmt == "e4m3":
        byte = np.frexp(amax)[1] - 1 + 127 - 7
    else:
        mant, ex = np.frexp(amax / 6.0)
        byte = np.where(mant > 0.5, ex, ex - 1) + 127
    byte = np.clip(np.where(amax > 0, byte, 1), 1, 254)
    scaled = (w * np.exp2(127.0 - byte)[:, None, :]).reshape(k, n).astype(np.float32)
    by_word = np.ascontiguousarray(scaled.reshape(k // 512, 128, 4, n).transpose(0, 1, 3, 2))
    if fmt == "e4m3":
        words = by_word.astype(ml_dtypes.float8_e4m3fn).view(np.uint8)
    else:
        c = by_word.astype(ml_dtypes.float4_e2m1fn).view(np.uint8) & 0xF
        words = (c[..., 0::2] | (c[..., 1::2] << 4)).reshape(k // 512, 128, 2 * n)
    return np.ascontiguousarray(words), np.ascontiguousarray(byte.astype(np.uint8).reshape(k // 512, 16, n))


def unpack_weight(words, scales, fmt):
    g, _, n = scales.shape
    words = np.ascontiguousarray(words).reshape(g, 128, n, -1)
    if fmt == "e4m3":
        vals = words.view(ml_dtypes.float8_e4m3fn).astype(np.float64)
    else:
        nib = np.empty((g, 128, n, 4), np.uint8)
        nib[..., 0::2] = words & 0xF
        nib[..., 1::2] = words >> 4
        vals = E2M1[nib]
    vals = vals * np.repeat(np.exp2(scales.astype(np.float64) - 127.0), 8, axis=1)[..., None]
    return vals.transpose(0, 1, 3, 2).reshape(g * 512, n)


K, T, J, R, O, N = 512, 512, 256, 512, 128, 256


def setup_inputs():
    n = np.random.standard_normal
    idx = np.random.permutation(T)[:J]
    idx2 = np.random.permutation(J)[:O]
    idx3 = np.random.permutation(J)[:O]
    fk = mx_kscale(K)
    fr = mx_kscale(R)
    xtp = pack_weight(n((K, T)) / fk[:, None], "e4m3")
    wp = pack_weight(n((K, R)) * 1 / np.sqrt(K) * fk[:, None] * fr, "e2m1")
    wbp = pack_weight(n((R, N)) * 1 / np.sqrt(R) / fr[:, None], "e2m1")
    return {
        "xt_words": xtp[0],
        "xt_scales": xtp[1],
        "w_words": wp[0],
        "w_scales": wp[1],
        "wb_words": wbp[0],
        "wb_scales": wbp[1],
        "rs": (1.0 * n((O, N))).astype(np.float32),
        "offs": striped(idx),
        "offs2": striped(idx2),
        "offs3": striped(idx3),
    }


def reference(xt_words, xt_scales, w_words, w_scales, wb_words, wb_scales, rs, offs, offs2, offs3):
    idx = unstriped(offs)
    idx2 = unstriped(offs2)
    idx3 = unstriped(offs3)
    xtu = unpack_weight(xt_words, xt_scales, "e4m3")
    wu = unpack_weight(w_words, w_scales, "e2m1")
    wbu = unpack_weight(wb_words, wb_scales, "e2m1")
    xtidxg = xtu[:, idx]
    a = wu.T @ xtidxg
    ha = np.maximum(a, 0.0)
    hid = ha[:, idx2] - ha[:, idx3]
    hidq = mxq(hid, 0, "e5m2")
    p = hidq.T @ wbu
    pk2 = np.max(np.abs(p), axis=1, keepdims=True)
    y = p / (pk2 + 0.2) + 0.3 * f64(rs)
    return y

@@ -1,0 +1,146 @@
+from contextlib import ExitStack
+
+import concourse.mybir as mybir
+
+K, T, J, R, O, N = 512, 512, 256, 512, 128, 256
+FLOPS = 2 * K * R * J + 2 * R * O * N
+
+F32 = mybir.dt.float32
+BF16 = mybir.dt.bfloat16
+I32 = mybir.dt.int32
+U32 = mybir.dt.uint32
+U16 = mybir.dt.uint16
+U8 = mybir.dt.uint8
+E4M3 = mybir.dt.float8_e4m3fn_x4
+E5M2 = mybir.dt.float8_e5m2_x4
+E2M1 = mybir.dt.float4_e2m1fn_x4
+ALU = mybir.AluOpType
+ACT = mybir.ActivationFunctionType
+
+P = 128
+PACK = 4
+
+
+def load_scale_rows(queue, plane, scales, q):
+    rows = scales[0].bitcast(I32)[4 * q : 4 * q + 4, :]
+    repeated = rows.unsqueeze(0).to_broadcast([8, 4, rows.shape[1]])
+    queue.dma_start(out=plane[32 * q : 32 * q + 32, :].bitcast(I32), in_=repeated)
+
+
+def tile_list_looks_picked_gap_rowpeaks_kernel(
+    tc, xt_words, xt_scales, w_words, w_scales, wb_words, wb_scales, rs, offs, offs2, offs3, out
+):
+    nc = tc.nc
+    with ExitStack() as ctx:
+        sb = ctx.enter_context(tc.tile_pool(name="sb", bufs=1))
+        ps = ctx.enter_context(tc.psum_pool(name="ps", bufs=1))
+
+        list1 = sb.tile([P, J // 16], U16, name="list1")
+        list2 = sb.tile([P, O // 16], U16, name="list2")
+        list3 = sb.tile([P, O // 16], U16, name="list3")
+        xw = sb.tile([P, T], I32, name="xw", align_bytes=64)
+        xs = sb.tile([P, T], U8, name="xs", align_bytes=64)
+        ww = sb.tile([P, 2 * R], U8, name="ww", align_bytes=64)
+        ws = sb.tile([P, R], U8, name="ws", align_bytes=64)
+        bw = sb.tile([P, 2 * N], U8, name="bw", align_bytes=64)
+        bs = sb.tile([P, N], U8, name="bs", align_bytes=64)
+        res = sb.tile([P, N], F32, name="res", align_bytes=64)
+
+        nc.sync.dma_start(list1[:], offs)
+        load_scale_rows(nc.scalar, xs, xt_scales, 0)
+        load_scale_rows(nc.sync, ws, w_scales, 0)
+        load_scale_rows(nc.scalar, xs, xt_scales, 1)
+        nc.sync.dma_start(out=xw[:], in_=xt_words[0].rearrange("p c r -> p (c r)").bitcast(I32))
+        load_scale_rows(nc.scalar, xs, xt_scales, 2)
+        nc.sync.dma_start(out=ww[:].bitcast(I32), in_=w_words[0].bitcast(I32))
+        load_scale_rows(nc.scalar, xs, xt_scales, 3)
+        for q in range(1, 4):
+            load_scale_rows(nc.sync, ws, w_scales, q)
+        nc.sync.dma_start(list2[:], offs2)
+        nc.sync.dma_start(list3[:], offs3)
+        nc.sync.dma_start(out=bw[:].bitcast(I32), in_=wb_words[0].bitcast(I32))
+        for q in range(4):
+            load_scale_rows(nc.sync, bs, wb_scales, q)
+        nc.sync.dma_start(out=res[:], in_=rs)
+
+        xsg = sb.tile([P, J], U8, name="xsg", align_bytes=64)
+        xwg = sb.tile([P, J], U32, name="xwg", align_bytes=64)
+        nc.vector.tensor_copy(xsg[:], xs[:].indirect(list1[:]))
+        nc.vector.tensor_copy(xwg[:], xw[:].bitcast(U32).indirect(list1[:]))
+
+        wwd = sb.tile([P, 2 * R], U8, name="wwd", align_bytes=64)
+        wsd = sb.tile([P, R], U8, name="wsd", align_bytes=64)
+        nc.vector.tensor_copy(
+            out=wwd[:].bitcast(U16).rearrange("p (t c i) -> p c t i", t=PACK, i=8),
+            in_=ww[:].bitcast(U16).rearrange("p (c i t) -> p c t i", t=PACK, i=8),
+        )
+        nc.vector.tensor_copy(
+            out=wsd[:].rearrange("p (t c i) -> p c t i", t=PACK, i=16),
+            in_=ws[:].rearrange("p (c i t) -> p c t i", t=PACK, i=16),
+        )
+
+        g2 = sb.tile([P, PACK, O], F32, name="g2", align_bytes=64)
+        g3 = sb.tile([P, PACK, O], F32, name="g3", align_bytes=64)
+        has = []
+        for t in range(PACK):
+            acc = ps.tile([P, J], F32, name="acc%d" % t)
+            nc.tensor.matmul_mx(
+                out=acc[:],
+                lhsT=wwd[:, 2 * P * t : 2 * P * (t + 1)].bitcast(E2M1),
+                lhsT_scale=wsd[:, P * t : P * (t + 1)],
+                rhs=xwg[:].bitcast(E4M3),
+                rhs_scale=xsg[:],
+                start=True,
+                stop=True,
+            )
+            ha = sb.tile([P, J], F32, name="ha%d" % t, align_bytes=64)
+            if t % 2 == 0:
+                nc.vector.tensor_scalar_max(ha[:], acc[:], 0.0)
+            else:
+                nc.scalar.activation(ha[:], acc[:], ACT.Relu)
+            has.append(ha)
+        for t in range(PACK):
+            for g, lst in ((g2, list2), (g3, list3)):
+                if t % 2 == 0:
+                    nc.vector.tensor_copy(g[:, t, :], has[t][:].indirect(lst[:]))
+                else:
+                    nc.scalar.activation(g[:, t, :], has[t][:].indirect(lst[:]), ACT.Copy)
+
+        hid = sb.tile([P, O * PACK], BF16, name="hid", align_bytes=64)
+        nc.vector.tensor_tensor(
+            out=hid[:].rearrange("p (c i t) -> p c t i", t=PACK, i=4),
+            in0=g2[:].rearrange("p t (c i) -> p c t i", i=4),
+            in1=g3[:].rearrange("p t (c i) -> p c t i", i=4),
+            op=ALU.subtract,
+        )
+        hw = sb.tile([P, O], U32, name="hw", align_bytes=64)
+        hs = sb.tile([P, O], U8, name="hs", align_bytes=64)
+        nc.vector.quantize_mx(out=hw[:].bitcast(E5M2), scales=hs[:], in_=hid[:])
+
+        res3 = sb.tile([P, N], F32, name="res3", align_bytes=64)
+        nc.scalar.activation(res3[:], res[:], ACT.Copy, scale=0.3)
+
+        prod = ps.tile([P, N], F32, name="prod")
+        nc.tensor.matmul_mx(
+            out=prod[:],
+            lhsT=hw[:].bitcast(E5M2),
+            lhsT_scale=hs[:],
+            rhs=bw[:].bitcast(E2M1),
+            rhs_scale=bs[:],
+            start=True,
+            stop=True,
+        )
+        mag = sb.tile([P, N], F32, name="mag", align_bytes=64)
+        nc.scalar.activation(mag[:], prod[:], ACT.Abs)
+        shifted = sb.tile([P, N], F32, name="shifted", align_bytes=64)
+        den = sb.tile([P, 1], F32, name="den")
+        nc.vector.tensor_scalar(
+            out=shifted[:], in0=mag[:], scalar1=0.2, scalar2=None, op0=ALU.add, op1=ALU.max, accum_out=den[:]
+        )
+        inv = sb.tile([P, 1], F32, name="inv")
+        nc.vector.reciprocal(inv[:], den[:])
+        y = sb.tile([P, N], F32, name="y", align_bytes=64)
+        nc.vector.scalar_tensor_tensor(
+            out=y[:], in0=prod[:], scalar=inv[:], in1=res3[:], op0=ALU.mult, op1=ALU.add
+        )
+        nc.sync.dma_start(out=out, in_=y[:])

@@ -47,15 +47,16 @@ def tile_list_looks_picked_gap_rowpeaks_kernel(
         res = sb.tile([P, N], F32, name="res", align_bytes=64)
 
         nc.sync.dma_start(list1[:], offs)
-        load_scale_rows(nc.scalar, xs, xt_scales, 0)
-        load_scale_rows(nc.sync, ws, w_scales, 0)
         load_scale_rows(nc.scalar, xs, xt_scales, 1)
-        nc.sync.dma_start(out=xw[:], in_=xt_words[0].rearrange("p c r -> p (c r)").bitcast(I32))
+        load_scale_rows(nc.sync, xs, xt_scales, 0)
         load_scale_rows(nc.scalar, xs, xt_scales, 2)
-        nc.sync.dma_start(out=ww[:].bitcast(I32), in_=w_words[0].bitcast(I32))
+        load_scale_rows(nc.sync, ws, w_scales, 0)
         load_scale_rows(nc.scalar, xs, xt_scales, 3)
-        for q in range(1, 4):
-            load_scale_rows(nc.sync, ws, w_scales, q)
+        nc.sync.dma_start(out=xw[:], in_=xt_words[0].rearrange("p c r -> p (c r)").bitcast(I32))
+        nc.sync.dma_start(out=ww[:].bitcast(I32), in_=w_words[0].bitcast(I32))
+        load_scale_rows(nc.gpsimd, ws, w_scales, 3)
+        load_scale_rows(nc.scalar, ws, w_scales, 1)
+        load_scale_rows(nc.sync, ws, w_scales, 2)
         nc.sync.dma_start(list2[:], offs2)
         nc.sync.dma_start(list3[:], offs3)
         nc.sync.dma_start(out=bw[:].bitcast(I32), in_=wb_words[0].bitcast(I32))
@@ -69,78 +70,96 @@ def tile_list_looks_picked_gap_rowpeaks_kernel(
         nc.vector.tensor_copy(xwg[:], xw[:].bitcast(U32).indirect(list1[:]))
 
         wwd = sb.tile([P, 2 * R], U8, name="wwd", align_bytes=64)
-        wsd = sb.tile([P, R], U8, name="wsd", align_bytes=64)
+        wsd_first = sb.tile([P, P], U8, name="wsd_first", align_bytes=64)
+        wsd_rest = sb.tile([P, R - P], U8, name="wsd_rest", align_bytes=64)
         nc.vector.tensor_copy(
             out=wwd[:].bitcast(U16).rearrange("p (t c i) -> p c t i", t=PACK, i=8),
             in_=ww[:].bitcast(U16).rearrange("p (c i t) -> p c t i", t=PACK, i=8),
         )
+        ws_dealt = ws[:].rearrange("p (c i t) -> p c t i", t=PACK, i=16)
+        nc.vector.tensor_copy(out=wsd_first[:].rearrange("p (c i) -> p c i", i=16), in_=ws_dealt[:, :, 0, :])
         nc.vector.tensor_copy(
-            out=wsd[:].rearrange("p (t c i) -> p c t i", t=PACK, i=16),
-            in_=ws[:].rearrange("p (c i t) -> p c t i", t=PACK, i=16),
+            out=wsd_rest[:].rearrange("p (t c i) -> p c t i", t=PACK - 1, i=16), in_=ws_dealt[:, :, 1:PACK, :]
         )
+        wsd = [wsd_first[:]] + [wsd_rest[:, P * u : P * (u + 1)] for u in range(PACK - 1)]
 
         g2 = sb.tile([P, PACK, O], F32, name="g2", align_bytes=64)
         g3 = sb.tile([P, PACK, O], F32, name="g3", align_bytes=64)
-        has = []
+        accs = [ps.tile([P, J], F32, name="acc%d" % t) for t in range(PACK)]
+        has = [sb.tile([P, J], F32, name="ha%d" % t, align_bytes=64) for t in range(PACK)]
         for t in range(PACK):
-            acc = ps.tile([P, J], F32, name="acc%d" % t)
             nc.tensor.matmul_mx(
-                out=acc[:],
+                out=accs[t][:],
                 lhsT=wwd[:, 2 * P * t : 2 * P * (t + 1)].bitcast(E2M1),
-                lhsT_scale=wsd[:, P * t : P * (t + 1)],
+                lhsT_scale=wsd[t],
                 rhs=xwg[:].bitcast(E4M3),
                 rhs_scale=xsg[:],
                 start=True,
                 stop=True,
             )
-            ha = sb.tile([P, J], F32, name="ha%d" % t, align_bytes=64)
-            if t % 2 == 0:
-                nc.vector.tensor_scalar_max(ha[:], acc[:], 0.0)
-            else:
-                nc.scalar.activation(ha[:], acc[:], ACT.Relu)
-            has.append(ha)
-        for t in range(PACK):
-            for g, lst in ((g2, list2), (g3, list3)):
-                if t % 2 == 0:
-                    nc.vector.tensor_copy(g[:, t, :], has[t][:].indirect(lst[:]))
-                else:
-                    nc.scalar.activation(g[:, t, :], has[t][:].indirect(lst[:]), ACT.Copy)
 
-        hid = sb.tile([P, O * PACK], BF16, name="hid", align_bytes=64)
-        nc.vector.tensor_tensor(
-            out=hid[:].rearrange("p (c i t) -> p c t i", t=PACK, i=4),
-            in0=g2[:].rearrange("p t (c i) -> p c t i", i=4),
-            in1=g3[:].rearrange("p t (c i) -> p c t i", i=4),
-            op=ALU.subtract,
-        )
+        def look_vector(g, lst, t):
+            nc.vector.tensor_copy(g[:, t, :], has[t][:].indirect(lst[:]))
+
+        def look_scalar(g, lst, t):
+            nc.scalar.activation(g[:, t, :], has[t][:].indirect(lst[:]), ACT.Copy)
+
+        nc.vector.tensor_scalar_max(has[0][:], accs[0][:], 0.0)
+        nc.scalar.activation(has[1][:], accs[1][:], ACT.Relu)
+        look_vector(g2, list2, 0)
+        look_scalar(g3, list3, 0)
+        nc.vector.tensor_scalar_max(has[2][:], accs[2][:], 0.0)
+        nc.scalar.activation(has[3][:], accs[3][:], ACT.Relu)
+        look_vector(g2, list2, 1)
+        look_scalar(g3, list3, 1)
+        look_vector(g2, list2, 2)
+        look_scalar(g2, list2, 3)
+        look_vector(g3, list3, 2)
+        look_scalar(g3, list3, 3)
+
+        H = O // 2
+        hid = [sb.tile([P, H * PACK], BF16, name="hid%d" % h, align_bytes=64) for h in range(2)]
+        for h in range(2):
+            nc.vector.tensor_tensor(
+                out=hid[h][:].rearrange("p (c i t) -> p c t i", t=PACK, i=4),
+                in0=g2[:, :, H * h : H * (h + 1)].rearrange("p t (c i) -> p c t i", i=4),
+                in1=g3[:, :, H * h : H * (h + 1)].rearrange("p t (c i) -> p c t i", i=4),
+                op=ALU.subtract,
+            )
         hw = sb.tile([P, O], U32, name="hw", align_bytes=64)
         hs = sb.tile([P, O], U8, name="hs", align_bytes=64)
-        nc.vector.quantize_mx(out=hw[:].bitcast(E5M2), scales=hs[:], in_=hid[:])
+        for h in range(2):
+            nc.vector.quantize_mx(
+                out=hw[:, H * h : H * (h + 1)].bitcast(E5M2), scales=hs[:, H * h : H * (h + 1)], in_=hid[h][:]
+            )
 
         res3 = sb.tile([P, N], F32, name="res3", align_bytes=64)
         nc.scalar.activation(res3[:], res[:], ACT.Copy, scale=0.3)
 
-        prod = ps.tile([P, N], F32, name="prod")
-        nc.tensor.matmul_mx(
-            out=prod[:],
-            lhsT=hw[:].bitcast(E5M2),
-            lhsT_scale=hs[:],
-            rhs=bw[:].bitcast(E2M1),
-            rhs_scale=bs[:],
-            start=True,
-            stop=True,
-        )
+        NH = N // 2
+        prod = [ps.tile([P, NH], F32, name="prod%d" % h) for h in range(2)]
         mag = sb.tile([P, N], F32, name="mag", align_bytes=64)
-        nc.scalar.activation(mag[:], prod[:], ACT.Abs)
         shifted = sb.tile([P, N], F32, name="shifted", align_bytes=64)
         den = sb.tile([P, 1], F32, name="den")
+        for h in range(2):
+            nc.tensor.matmul_mx(
+                out=prod[h][:],
+                lhsT=hw[:].bitcast(E5M2),
+                lhsT_scale=hs[:],
+                rhs=bw[:, 2 * NH * h : 2 * NH * (h + 1)].bitcast(E2M1),
+                rhs_scale=bs[:, NH * h : NH * (h + 1)],
+                start=True,
+                stop=True,
+            )
+            nc.scalar.activation(mag[:, NH * h : NH * (h + 1)], prod[h][:], ACT.Abs)
         nc.vector.tensor_scalar(
             out=shifted[:], in0=mag[:], scalar1=0.2, scalar2=None, op0=ALU.add, op1=ALU.max, accum_out=den[:]
         )
         inv = sb.tile([P, 1], F32, name="inv")
         nc.vector.reciprocal(inv[:], den[:])
-        y = sb.tile([P, N], F32, name="y", align_bytes=64)
-        nc.vector.scalar_tensor_tensor(
-            out=y[:], in0=prod[:], scalar=inv[:], in1=res3[:], op0=ALU.mult, op1=ALU.add
-        )
-        nc.sync.dma_start(out=out, in_=y[:])
+        for h, queue in enumerate((nc.sync, nc.scalar)):
+            y = sb.tile([P, NH], F32, name="y%d" % h, align_bytes=64)
+            nc.vector.scalar_tensor_tensor(
+                out=y[:], in0=prod[h][:], scalar=inv[:], in1=res3[:, NH * h : NH * (h + 1)], op0=ALU.mult, op1=ALU.add
+            )
+            queue.dma_start(out=out[:, NH * h : NH * (h + 1)], in_=y[:])

@@ -54,9 +54,8 @@ def tile_list_looks_picked_gap_rowpeaks_kernel(
         load_scale_rows(nc.scalar, xs, xt_scales, 3)
         nc.sync.dma_start(out=xw[:], in_=xt_words[0].rearrange("p c r -> p (c r)").bitcast(I32))
         nc.sync.dma_start(out=ww[:].bitcast(I32), in_=w_words[0].bitcast(I32))
-        load_scale_rows(nc.gpsimd, ws, w_scales, 3)
-        load_scale_rows(nc.scalar, ws, w_scales, 1)
-        load_scale_rows(nc.sync, ws, w_scales, 2)
+        for q in range(1, 4):
+            load_scale_rows(nc.sync, ws, w_scales, q)
         nc.sync.dma_start(list2[:], offs2)
         nc.sync.dma_start(list3[:], offs3)
         nc.sync.dma_start(out=bw[:].bitcast(I32), in_=wb_words[0].bitcast(I32))
@@ -133,7 +132,7 @@ def tile_list_looks_picked_gap_rowpeaks_kernel(
                 out=hw[:, H * h : H * (h + 1)].bitcast(E5M2), scales=hs[:, H * h : H * (h + 1)], in_=hid[h][:]
             )
 
-        res3 = sb.tile([P, N], F32, name="res3", align_bytes=64)
+        res3 = sb.tile([P, N], F32, name="ha3", align_bytes=64)
         nc.scalar.activation(res3[:], res[:], ACT.Copy, scale=0.3)
 
         NH = N // 2

@@ -22,9 +22,7 @@ PACK = 4
 
 
 def load_scale_rows(queue, plane, scales, q):
-    rows = scales[0].bitcast(I32)[4 * q : 4 * q + 4, :]
-    repeated = rows.unsqueeze(0).to_broadcast([8, 4, rows.shape[1]])
-    queue.dma_start(out=plane[32 * q : 32 * q + 32, :].bitcast(I32), in_=repeated)
+    queue.dma_start(out=plane[32 * q : 32 * q + 4, :].bitcast(I32), in_=scales[0].bitcast(I32)[4 * q : 4 * q + 4, :])
 
 
 def tile_list_looks_picked_gap_rowpeaks_kernel(
@@ -46,14 +44,15 @@ def tile_list_looks_picked_gap_rowpeaks_kernel(
         bs = sb.tile([P, N], U8, name="bs", align_bytes=64)
         res = sb.tile([P, N], F32, name="res", align_bytes=64)
 
+        nc.gpsimd.memset(xs[:].bitcast(I32), 0)
+        for plane in (ws, bs):
+            nc.vector.memset(plane[:].bitcast(I32), 0)
         nc.sync.dma_start(list1[:], offs)
-        load_scale_rows(nc.scalar, xs, xt_scales, 1)
-        load_scale_rows(nc.sync, xs, xt_scales, 0)
-        load_scale_rows(nc.scalar, xs, xt_scales, 2)
-        load_scale_rows(nc.sync, ws, w_scales, 0)
-        load_scale_rows(nc.scalar, xs, xt_scales, 3)
-        nc.sync.dma_start(out=xw[:], in_=xt_words[0].rearrange("p c r -> p (c r)").bitcast(I32))
         nc.sync.dma_start(out=ww[:].bitcast(I32), in_=w_words[0].bitcast(I32))
+        for q in range(4):
+            load_scale_rows(nc.scalar if q % 2 else nc.sync, xs, xt_scales, q)
+        nc.sync.dma_start(out=xw[:], in_=xt_words[0].rearrange("p c r -> p (c r)").bitcast(I32))
+        load_scale_rows(nc.scalar, ws, w_scales, 0)
         for q in range(1, 4):
             load_scale_rows(nc.sync, ws, w_scales, q)
         nc.sync.dma_start(list2[:], offs2)
@@ -63,11 +62,6 @@ def tile_list_looks_picked_gap_rowpeaks_kernel(
             load_scale_rows(nc.sync, bs, wb_scales, q)
         nc.sync.dma_start(out=res[:], in_=rs)
 
-        xsg = sb.tile([P, J], U8, name="xsg", align_bytes=64)
-        xwg = sb.tile([P, J], U32, name="xwg", align_bytes=64)
-        nc.vector.tensor_copy(xsg[:], xs[:].indirect(list1[:]))
-        nc.vector.tensor_copy(xwg[:], xw[:].bitcast(U32).indirect(list1[:]))
-
         wwd = sb.tile([P, 2 * R], U8, name="wwd", align_bytes=64)
         wsd_first = sb.tile([P, P], U8, name="wsd_first", align_bytes=64)
         wsd_rest = sb.tile([P, R - P], U8, name="wsd_rest", align_bytes=64)
@@ -75,6 +69,11 @@ def tile_list_looks_picked_gap_rowpeaks_kernel(
             out=wwd[:].bitcast(U16).rearrange("p (t c i) -> p c t i", t=PACK, i=8),
             in_=ww[:].bitcast(U16).rearrange("p (c i t) -> p c t i", t=PACK, i=8),
         )
+        xsg = sb.tile([P, J], U8, name="xsg", align_bytes=64)
+        xwg = sb.tile([P, J], U32, name="xwg", align_bytes=64)
+        nc.vector.tensor_copy(xsg[:], xs[:].indirect(list1[:]))
+        nc.vector.tensor_copy(xwg[:], xw[:].bitcast(U32).indirect(list1[:]))
+
         ws_dealt = ws[:].rearrange("p (c i t) -> p c t i", t=PACK, i=16)
         nc.vector.tensor_copy(out=wsd_first[:].rearrange("p (c i) -> p c i", i=16), in_=ws_dealt[:, :, 0, :])
         nc.vector.tensor_copy(

from contextlib import ExitStack

import concourse.mybir as mybir

K, T, J, R, O, N = 512, 512, 256, 512, 128, 256
FLOPS = 2 * K * R * J + 2 * R * O * N

F32 = mybir.dt.float32
BF16 = mybir.dt.bfloat16
I32 = mybir.dt.int32
U32 = mybir.dt.uint32
U16 = mybir.dt.uint16
U8 = mybir.dt.uint8
E4M3 = mybir.dt.float8_e4m3fn_x4
E5M2 = mybir.dt.float8_e5m2_x4
E2M1 = mybir.dt.float4_e2m1fn_x4
ALU = mybir.AluOpType
ACT = mybir.ActivationFunctionType

P = 128
PACK = 4


def load_scale_rows(queue, plane, scales, q):
    queue.dma_start(out=plane[32 * q : 32 * q + 4, :].bitcast(I32), in_=scales[0].bitcast(I32)[4 * q : 4 * q + 4, :])


def tile_list_looks_picked_gap_rowpeaks_kernel(
    tc, xt_words, xt_scales, w_words, w_scales, wb_words, wb_scales, rs, offs, offs2, offs3, out
):
    nc = tc.nc
    with ExitStack() as ctx:
        sb = ctx.enter_context(tc.tile_pool(name="sb", bufs=1))
        ps = ctx.enter_context(tc.psum_pool(name="ps", bufs=1))

        list1 = sb.tile([P, J // 16], U16, name="list1")
        list2 = sb.tile([P, O // 16], U16, name="list2")
        list3 = sb.tile([P, O // 16], U16, name="list3")
        xw = sb.tile([P, T], I32, name="xw", align_bytes=64)
        xs = sb.tile([P, T], U8, name="xs", align_bytes=64)
        ww = sb.tile([P, 2 * R], U8, name="ww", align_bytes=64)
        ws = sb.tile([P, R], U8, name="ws", align_bytes=64)
        bw = sb.tile([P, 2 * N], U8, name="bw", align_bytes=64)
        bs = sb.tile([P, N], U8, name="bs", align_bytes=64)
        res = sb.tile([P, N], F32, name="res", align_bytes=64)

        nc.gpsimd.memset(xs[:].bitcast(I32), 0)
        for plane in (ws, bs):
            nc.vector.memset(plane[:].bitcast(I32), 0)
        nc.sync.dma_start(list1[:], offs)
        nc.sync.dma_start(out=ww[:].bitcast(I32), in_=w_words[0].bitcast(I32))
        for q in range(4):
            load_scale_rows(nc.scalar if q % 2 else nc.sync, xs, xt_scales, q)
        nc.sync.dma_start(out=xw[:], in_=xt_words[0].rearrange("p c r -> p (c r)").bitcast(I32))
        load_scale_rows(nc.scalar, ws, w_scales, 0)
        for q in range(1, 4):
            load_scale_rows(nc.sync, ws, w_scales, q)
        nc.sync.dma_start(list2[:], offs2)
        nc.sync.dma_start(list3[:], offs3)
        nc.sync.dma_start(out=bw[:].bitcast(I32), in_=wb_words[0].bitcast(I32))
        for q in range(4):
            load_scale_rows(nc.sync, bs, wb_scales, q)
        nc.sync.dma_start(out=res[:], in_=rs)

        wwd = sb.tile([P, 2 * R], U8, name="wwd", align_bytes=64)
        wsd_first = sb.tile([P, P], U8, name="wsd_first", align_bytes=64)
        wsd_rest = sb.tile([P, R - P], U8, name="wsd_rest", align_bytes=64)
        nc.vector.tensor_copy(
            out=wwd[:].bitcast(U16).rearrange("p (t c i) -> p c t i", t=PACK, i=8),
            in_=ww[:].bitcast(U16).rearrange("p (c i t) -> p c t i", t=PACK, i=8),
        )
        xsg = sb.tile([P, J], U8, name="xsg", align_bytes=64)
        xwg = sb.tile([P, J], U32, name="xwg", align_bytes=64)
        nc.vector.tensor_copy(xsg[:], xs[:].indirect(list1[:]))
        nc.vector.tensor_copy(xwg[:], xw[:].bitcast(U32).indirect(list1[:]))

        ws_dealt = ws[:].rearrange("p (c i t) -> p c t i", t=PACK, i=16)
        nc.vector.tensor_copy(out=wsd_first[:].rearrange("p (c i) -> p c i", i=16), in_=ws_dealt[:, :, 0, :])
        nc.vector.tensor_copy(
            out=wsd_rest[:].rearrange("p (t c i) -> p c t i", t=PACK - 1, i=16), in_=ws_dealt[:, :, 1:PACK, :]
        )
        wsd = [wsd_first[:]] + [wsd_rest[:, P * u : P * (u + 1)] for u in range(PACK - 1)]

        g2 = sb.tile([P, PACK, O], F32, name="g2", align_bytes=64)
        g3 = sb.tile([P, PACK, O], F32, name="g3", align_bytes=64)
        accs = [ps.tile([P, J], F32, name="acc%d" % t) for t in range(PACK)]
        has = [sb.tile([P, J], F32, name="ha%d" % t, align_bytes=64) for t in range(PACK)]
        for t in range(PACK):
            nc.tensor.matmul_mx(
                out=accs[t][:],
                lhsT=wwd[:, 2 * P * t : 2 * P * (t + 1)].bitcast(E2M1),
                lhsT_scale=wsd[t],
                rhs=xwg[:].bitcast(E4M3),
                rhs_scale=xsg[:],
                start=True,
                stop=True,
            )

        def look_vector(g, lst, t):
            nc.vector.tensor_copy(g[:, t, :], has[t][:].indirect(lst[:]))

        def look_scalar(g, lst, t):
            nc.scalar.activation(g[:, t, :], has[t][:].indirect(lst[:]), ACT.Copy)

        nc.vector.tensor_scalar_max(has[0][:], accs[0][:], 0.0)
        nc.scalar.activation(has[1][:], accs[1][:], ACT.Relu)
        look_vector(g2, list2, 0)
        look_scalar(g3, list3, 0)
        nc.vector.tensor_scalar_max(has[2][:], accs[2][:], 0.0)
        nc.scalar.activation(has[3][:], accs[3][:], ACT.Relu)
        look_vector(g2, list2, 1)
        look_scalar(g3, list3, 1)
        look_vector(g2, list2, 2)
        look_scalar(g2, list2, 3)
        look_vector(g3, list3, 2)
        look_scalar(g3, list3, 3)

        H = O // 2
        hid = [sb.tile([P, H * PACK], BF16, name="hid%d" % h, align_bytes=64) for h in range(2)]
        for h in range(2):
            nc.vector.tensor_tensor(
                out=hid[h][:].rearrange("p (c i t) -> p c t i", t=PACK, i=4),
                in0=g2[:, :, H * h : H * (h + 1)].rearrange("p t (c i) -> p c t i", i=4),
                in1=g3[:, :, H * h : H * (h + 1)].rearrange("p t (c i) -> p c t i", i=4),
                op=ALU.subtract,
            )
        hw = sb.tile([P, O], U32, name="hw", align_bytes=64)
        hs = sb.tile([P, O], U8, name="hs", align_bytes=64)
        for h in range(2):
            nc.vector.quantize_mx(
                out=hw[:, H * h : H * (h + 1)].bitcast(E5M2), scales=hs[:, H * h : H * (h + 1)], in_=hid[h][:]
            )

        res3 = sb.tile([P, N], F32, name="ha3", align_bytes=64)
        nc.scalar.activation(res3[:], res[:], ACT.Copy, scale=0.3)

        NH = N // 2
        prod = [ps.tile([P, NH], F32, name="prod%d" % h) for h in range(2)]
        mag = sb.tile([P, N], F32, name="mag", align_bytes=64)
        shifted = sb.tile([P, N], F32, name="shifted", align_bytes=64)
        den = sb.tile([P, 1], F32, name="den")
        for h in range(2):
            nc.tensor.matmul_mx(
                out=prod[h][:],
                lhsT=hw[:].bitcast(E5M2),
                lhsT_scale=hs[:],
                rhs=bw[:, 2 * NH * h : 2 * NH * (h + 1)].bitcast(E2M1),
                rhs_scale=bs[:, NH * h : NH * (h + 1)],
                start=True,
                stop=True,
            )
            nc.scalar.activation(mag[:, NH * h : NH * (h + 1)], prod[h][:], ACT.Abs)
        nc.vector.tensor_scalar(
            out=shifted[:], in0=mag[:], scalar1=0.2, scalar2=None, op0=ALU.add, op1=ALU.max, accum_out=den[:]
        )
        inv = sb.tile([P, 1], F32, name="inv")
        nc.vector.reciprocal(inv[:], den[:])
        for h, queue in enumerate((nc.sync, nc.scalar)):
            y = sb.tile([P, NH], F32, name="y%d" % h, align_bytes=64)
            nc.vector.scalar_tensor_tensor(
                out=y[:], in0=prod[h][:], scalar=inv[:], in1=res3[:, NH * h : NH * (h + 1)], op0=ALU.mult, op1=ALU.add
            )
            queue.dma_start(out=out[:, NH * h : NH * (h + 1)], in_=y[:])
